import numpy as np, ml_dtypes
CORES = [10,34,74,98]
N = 4
K, F = 4, 64
def setup_inputs(rng):
    return {"gr": rng.standard_normal((N, K, 128, N * F), dtype=np.float32).astype(ml_dtypes.bfloat16)}
def setup_inputs_big(rng):
    d = setup_inputs(rng)
    for k in ("gr",): d[k] = (d[k].astype(np.float32) * 1048576.0).astype(d[k].dtype)
    return d
def setup_inputs_small(rng):
    d = setup_inputs(rng)
    for k in ("gr",): d[k] = (d[k].astype(np.float32) * (1 / 1048576.0)).astype(d[k].dtype)
    return d
def reference(gr):
    s = gr.astype(np.float64).sum(axis=(0, 1))
    return {"y": np.stack([s[:, F * r:F * r + F] for r in range(N)]).astype(np.float32 if gr.dtype != np.float64 else np.float64)}

@@ -1,0 +1,110 @@
+from concourse.bass import DstId, RemoteDMATransfer
+from concourse.mybir import AluOpType
+
+N, K, F = 4, 4, 64
+W = N * F
+
+SCRATCH = {
+    "tab": ("sbuf", [128, K * W], "bfloat16"),
+    "p1": ("psum", [128, W], "float32"),
+    "p2": ("psum", [128, W], "float32"),
+    "part": ("sbuf", [128, W], "float32"),
+    "acc": ("psum", [128, (N - 1) * F], "float32"),
+    "land": ("sbuf", [128, (N - 1) * F], "float32"),
+    "res": ("sbuf", [128, F], "float32"),
+}
+SEMAPHORES = ["ld01", "ld2", "ld3", "v1", "v2", "rdy0", "rdy1", "own", "arr0", "arr1", "arr2", "a0", "a1",
+              "done", "stored", "sent"]
+
+
+def _hops(topo, a, b):
+    ca, cb = topo.chip(a), topo.chip(b)
+    if ca == cb:
+        return 0
+    return 1 if (topo.mates(ca, cb) or topo.same_plane(ca, cb)) else 2
+
+
+def _order(topo, cores, r):
+    n = len(cores)
+    return sorted([(r + d) % n for d in range(1, n)], key=lambda q: -_hops(topo, cores[r], cores[q]))
+
+
+def _engines(topo, cores, r):
+    m = -1
+    for q in range(len(cores)):
+        if q != r:
+            m &= topo.mask(cores[r], cores[q])
+    return [e for e in range(16) if (m >> e) & 1]
+
+
+def _plan(topo, cores, r):
+    a, b, c = _order(topo, cores, r)
+    eng = _engines(topo, cores, r)
+    h = len(eng) // 2
+    bits = lambda es: sum(1 << e for e in es)
+    return [(0, a, bits(eng[:h]), h), (0, b, bits(eng[h:]), len(eng) - h), (1, c, bits(eng), len(eng))]
+
+
+def rank_program(g, core, T, topo):
+    rank = T.rank_of(core)
+    if rank is None:
+        return
+    S, cores, v, add = T.sem, T.cores, g.vector, AluOpType.add
+
+    def tab(k):
+        return T.tab[:, k * W:(k + 1) * W]
+
+    def blk(t, q):
+        return t[:, q * F:(q + 1) * F]
+
+    def slot(dst, src):
+        return (src - dst) % N - 1
+
+    g.sync.dma_start(tab(0), T.gr[0]).then_inc(S.ld01, 16)
+    g.scalar.dma_start(tab(1), T.gr[1]).then_inc(S.ld01, 16)
+    g.sync.dma_start(tab(2), T.gr[2]).then_inc(S.ld2, 16)
+    g.scalar.dma_start(tab(3), T.gr[3]).then_inc(S.ld3, 16)
+
+    v.wait_ge(S.ld01, 32)
+    v.tensor_tensor(T.p1[:], tab(0), tab(1), add).then_inc(S.v1, 1)
+    v.wait_ge(S.ld2, 16)
+    v.wait_ge(S.v1, 1)
+    v.tensor_tensor(T.p2[:], T.p1[:], tab(2), add).then_inc(S.v2, 1)
+    v.wait_ge(S.ld3, 16)
+    v.wait_ge(S.v2, 1)
+    plan = _plan(topo, cores, rank)
+    for wave, q, _m, _n in plan:
+        v.tensor_tensor(blk(T.part, q), blk(T.p2, q), blk(tab(3), q), add).then_inc(S["rdy%d" % wave], 1)
+    v.tensor_tensor(blk(T.acc, 0), blk(T.p2, rank), blk(tab(3), rank), add).then_inc(S.own, 1)
+
+    sent = 0
+    for wave in (0, 1):
+        mine = [p for p in plan if p[0] == wave]
+        g.wait_ge(S["rdy%d" % wave], len(mine))
+        xs = []
+        for _w, q, m, n in mine:
+            rid, pid, _se = topo.addr(cores[q])
+            s = slot(q, rank)
+            xs.append(RemoteDMATransfer(dst_ids=[DstId(rid=rid, pnc=pid)], dma_engine_mask=m,
+                                        remote_sem=S["arr%d" % s], src=blk(T.part, q), dst=blk(T.land, s)))
+            sent += n
+        g.remote_dma_fused(xs, local_sem=S.sent)
+
+    inc = []
+    for r in range(N):
+        if r != rank:
+            inc += [(w, slot(rank, r), n) for w, q, _m, n in _plan(topo, cores, r) if q == rank]
+    inc.sort()
+    v.wait_ge(S.own, 1)
+    for i, (_w, s, n) in enumerate(inc):
+        v.wait_ge(S["arr%d" % s], n)
+        if i > 0:
+            v.wait_ge(S["a%d" % (i - 1)], 1)
+        if i < len(inc) - 1:
+            v.tensor_tensor(blk(T.acc, i + 1), blk(T.acc, i), blk(T.land, s), add).then_inc(S["a%d" % i], 1)
+        else:
+            v.tensor_tensor(T.res[:], blk(T.acc, i), blk(T.land, s), add).then_inc(S.done, 1)
+    g.sync.wait_ge(S.done, 1)
+    g.sync.dma_start(T.y[:], T.res[:]).then_inc(S.stored, 16)
+    g.sync.wait_ge(S.stored, 16)
+    g.wait_ge(S.sent, sent)

@@ -6,15 +6,17 @@ W = N * F
 
 SCRATCH = {
     "tab": ("sbuf", [128, K * W], "bfloat16"),
+    "p0": ("psum", [128, W], "float32"),
     "p1": ("psum", [128, W], "float32"),
     "p2": ("psum", [128, W], "float32"),
     "part": ("sbuf", [128, W], "float32"),
-    "acc": ("psum", [128, (N - 1) * F], "float32"),
+    "acc": ("psum", [128, N * F], "float32"),
+    "early": ("sbuf", [128, F], "bfloat16"),
     "land": ("sbuf", [128, (N - 1) * F], "float32"),
     "res": ("sbuf", [128, F], "float32"),
 }
-SEMAPHORES = ["ld01", "ld2", "ld3", "v1", "v2", "rdy0", "rdy1", "own", "arr0", "arr1", "arr2", "a0", "a1",
-              "done", "stored", "sent"]
+SEMAPHORES = ["ld0", "ld1", "ld2", "ld3", "v0", "v1", "v2", "rdy0", "rdy1", "o1", "o2", "own",
+              "arre", "arr0", "arr1", "arr2", "a0", "a1", "a2", "done", "stored", "sent"]
 
 
 def _hops(topo, a, b):
@@ -24,25 +26,21 @@ def _hops(topo, a, b):
     return 1 if (topo.mates(ca, cb) or topo.same_plane(ca, cb)) else 2
 
 
-def _order(topo, cores, r):
-    n = len(cores)
-    return sorted([(r + d) % n for d in range(1, n)], key=lambda q: -_hops(topo, cores[r], cores[q]))
-
-
 def _engines(topo, cores, r):
     m = -1
     for q in range(len(cores)):
         if q != r:
             m &= topo.mask(cores[r], cores[q])
-    return [e for e in range(16) if (m >> e) & 1]
+    return [e for e in range(m.bit_length()) if (m >> e) & 1]
 
 
 def _plan(topo, cores, r):
-    a, b, c = _order(topo, cores, r)
+    n = len(cores)
+    a, b, c = sorted([(r + d) % n for d in range(1, n)], key=lambda q: -_hops(topo, cores[r], cores[q]))
     eng = _engines(topo, cores, r)
     h = len(eng) // 2
     bits = lambda es: sum(1 << e for e in es)
-    return [(0, a, bits(eng[:h]), h), (0, b, bits(eng[h:]), len(eng) - h), (1, c, bits(eng), len(eng))]
+    return [(0, a, bits(eng[:h]), h), (0, c, bits(eng[h:]), len(eng) - h), (1, b, bits(eng), len(eng))]
 
 
 def rank_program(g, core, T, topo):
@@ -60,24 +58,38 @@ def rank_program(g, core, T, topo):
     def slot(dst, src):
         return (src - dst) % N - 1
 
-    g.sync.dma_start(tab(0), T.gr[0]).then_inc(S.ld01, 16)
-    g.scalar.dma_start(tab(1), T.gr[1]).then_inc(S.ld01, 16)
+    plan = _plan(topo, cores, rank)
+    first = plan[0][1]
+    allm, alln = plan[-1][2], plan[-1][3]
+
+    g.sync.dma_start(tab(0), T.gr[0]).then_inc(S.ld0, 16)
+    g.scalar.dma_start(tab(1), T.gr[1]).then_inc(S.ld1, 16)
     g.sync.dma_start(tab(2), T.gr[2]).then_inc(S.ld2, 16)
     g.scalar.dma_start(tab(3), T.gr[3]).then_inc(S.ld3, 16)
 
-    v.wait_ge(S.ld01, 32)
-    v.tensor_tensor(T.p1[:], tab(0), tab(1), add).then_inc(S.v1, 1)
+    rid, pid, _se = topo.addr(cores[first])
+    g.wait_ge(S.ld0, 16)
+    g.remote_dma(out_ap=T.early[:], in_ap=blk(tab(0), first), remote_sem=S.arre, local_sem=S.sent,
+                 pid=pid, routing_id=rid, dma_engine_mask=allm)
+    sent = alln
+
+    v.wait_ge(S.ld0, 16)
+    for _w, q, _m, _n in plan[1:]:
+        v.tensor_copy(blk(T.p0, q), blk(tab(0), q)).then_inc(S.v0, 1)
+    v.wait_ge(S.ld1, 16)
+    v.tensor_copy(blk(T.p1, first), blk(tab(1), first)).then_inc(S.v1, 1)
+    v.wait_ge(S.v0, N - 2)
+    for _w, q, _m, _n in plan[1:]:
+        v.tensor_tensor(blk(T.p1, q), blk(T.p0, q), blk(tab(1), q), add).then_inc(S.v1, 1)
     v.wait_ge(S.ld2, 16)
-    v.wait_ge(S.v1, 1)
-    v.tensor_tensor(T.p2[:], T.p1[:], tab(2), add).then_inc(S.v2, 1)
+    v.wait_ge(S.v1, N - 1)
+    for _w, q, _m, _n in plan:
+        v.tensor_tensor(blk(T.p2, q), blk(T.p1, q), blk(tab(2), q), add).then_inc(S.v2, 1)
     v.wait_ge(S.ld3, 16)
-    v.wait_ge(S.v2, 1)
-    plan = _plan(topo, cores, rank)
+    v.wait_ge(S.v2, N - 1)
     for wave, q, _m, _n in plan:
         v.tensor_tensor(blk(T.part, q), blk(T.p2, q), blk(tab(3), q), add).then_inc(S["rdy%d" % wave], 1)
-    v.tensor_tensor(blk(T.acc, 0), blk(T.p2, rank), blk(tab(3), rank), add).then_inc(S.own, 1)
 
-    sent = 0
     for wave in (0, 1):
         mine = [p for p in plan if p[0] == wave]
         g.wait_ge(S["rdy%d" % wave], len(mine))
@@ -90,20 +102,29 @@ def rank_program(g, core, T, topo):
             sent += n
         g.remote_dma_fused(xs, local_sem=S.sent)
 
+    v.tensor_tensor(blk(T.p1, rank), blk(tab(0), rank), blk(tab(1), rank), add).then_inc(S.o1, 1)
+    v.wait_ge(S.o1, 1)
+    v.tensor_tensor(blk(T.p2, rank), blk(T.p1, rank), blk(tab(2), rank), add).then_inc(S.o2, 1)
+    v.wait_ge(S.o2, 1)
+    v.tensor_tensor(blk(T.acc, 0), blk(T.p2, rank), blk(tab(3), rank), add).then_inc(S.own, 1)
+
     inc = []
     for r in range(N):
         if r != rank:
-            inc += [(w, slot(rank, r), n) for w, q, _m, n in _plan(topo, cores, r) if q == rank]
-    inc.sort()
+            pr = _plan(topo, cores, r)
+            if pr[0][1] == rank:
+                inc.append((-1, S.arre, pr[-1][3], T.early[:]))
+            inc += [(w, S["arr%d" % slot(rank, r)], n, blk(T.land, slot(rank, r))) for w, q, _m, n in pr if q == rank]
+    inc.sort(key=lambda x: x[0])
     v.wait_ge(S.own, 1)
-    for i, (_w, s, n) in enumerate(inc):
-        v.wait_ge(S["arr%d" % s], n)
+    for i, (_w, sem, n, ap) in enumerate(inc):
+        v.wait_ge(sem, n)
         if i > 0:
             v.wait_ge(S["a%d" % (i - 1)], 1)
         if i < len(inc) - 1:
-            v.tensor_tensor(blk(T.acc, i + 1), blk(T.acc, i), blk(T.land, s), add).then_inc(S["a%d" % i], 1)
+            v.tensor_tensor(blk(T.acc, i + 1), blk(T.acc, i), ap, add).then_inc(S["a%d" % i], 1)
         else:
-            v.tensor_tensor(T.res[:], blk(T.acc, i), blk(T.land, s), add).then_inc(S.done, 1)
+            v.tensor_tensor(T.res[:], blk(T.acc, i), ap, add).then_inc(S.done, 1)
     g.sync.wait_ge(S.done, 1)
     g.sync.dma_start(T.y[:], T.res[:]).then_inc(S.stored, 16)
     g.sync.wait_ge(S.stored, 16)

@@ -3,19 +3,29 @@ from concourse.mybir import AluOpType
 
 N, K, F = 4, 4, 64
 W = N * F
+G = 4
+PT = 128 // G
+KP = (K - 1) * PT
+WS = 128 + G - 1
 
 SCRATCH = {
-    "tab": ("sbuf", [128, K * W], "bfloat16"),
-    "p0": ("psum", [128, W], "float32"),
-    "p1": ("psum", [128, W], "float32"),
-    "p2": ("psum", [128, W], "float32"),
+    "t0": ("sbuf", [128, W], "bfloat16"),
+    "tab": ("sbuf", [128, G * W], "bfloat16"),
+    "ones": ("sbuf", [128, WS], "float32"),
+    "idx": ("sbuf", [128, WS], "float32"),
+    "tr": ("sbuf", [128, 32], "float32"),
+    "sel": ("sbuf", [128, WS], "bfloat16"),
+    "ps0": ("psum", [128, 512], "float32"),
+    "ps1": ("psum", [128, 512], "float32"),
+    "ps2": ("psum", [128, 512], "float32"),
+    "ps3": ("psum", [128, 512], "float32"),
     "part": ("sbuf", [128, W], "float32"),
     "acc": ("psum", [128, N * F], "float32"),
     "early": ("sbuf", [128, F], "bfloat16"),
     "land": ("sbuf", [128, (N - 1) * F], "float32"),
     "res": ("sbuf", [128, F], "float32"),
 }
-SEMAPHORES = ["ld0", "ld1", "ld2", "ld3", "v0", "v1", "v2", "rdy0", "rdy1", "o1", "o2", "own",
+SEMAPHORES = ["ld0", "ld1", "b0", "b1", "b2", "selr", "mm0", "mm1", "mm2", "mm3", "rdy0", "rdy1", "own",
               "arre", "arr0", "arr1", "arr2", "a0", "a1", "a2", "done", "stored", "sent"]
 
 
@@ -47,10 +57,7 @@ def rank_program(g, core, T, topo):
     rank = T.rank_of(core)
     if rank is None:
         return
-    S, cores, v, add = T.sem, T.cores, g.vector, AluOpType.add
-
-    def tab(k):
-        return T.tab[:, k * W:(k + 1) * W]
+    S, cores, v, pe, add = T.sem, T.cores, g.vector, g.tensor, AluOpType.add
 
     def blk(t, q):
         return t[:, q * F:(q + 1) * F]
@@ -62,33 +69,38 @@ def rank_program(g, core, T, topo):
     first = plan[0][1]
     allm, alln = plan[-1][2], plan[-1][3]
 
-    g.sync.dma_start(tab(0), T.gr[0]).then_inc(S.ld0, 16)
-    g.scalar.dma_start(tab(1), T.gr[1]).then_inc(S.ld1, 16)
-    g.sync.dma_start(tab(2), T.gr[2]).then_inc(S.ld2, 16)
-    g.scalar.dma_start(tab(3), T.gr[3]).then_inc(S.ld3, 16)
+    g.sync.dma_start(T.t0[:], T.gr[0]).then_inc(S.ld0, 16)
+    g.scalar.dma_start(T.tab[0:KP, :], T.gr[1:K]).then_inc(S.ld1, 16)
+
+    v.memset(T.ones[:], 1.0).then_inc(S.b0, 1)
+    v.wait_ge(S.b0, 1)
+    v.tensor_tensor_scan(T.idx[:], T.ones[:], T.ones[:], 0.0, AluOpType.mult, add).then_inc(S.b1, 1)
+    v.wait_ge(S.b1, 1)
+    v.transpose(T.tr[:], T.idx[:, 0:32]).then_inc(S.b2, 1)
+    v.wait_ge(S.b2, 1)
+    v.tensor_scalar(T.sel[:], T.idx[:], 1.0 / G, T.tr[:, 0:1], AluOpType.mult, AluOpType.is_equal).then_inc(S.selr, 1)
 
     rid, pid, _se = topo.addr(cores[first])
     g.wait_ge(S.ld0, 16)
-    g.remote_dma(out_ap=T.early[:], in_ap=blk(tab(0), first), remote_sem=S.arre, local_sem=S.sent,
+    g.remote_dma(out_ap=T.early[:], in_ap=blk(T.t0, first), remote_sem=S.arre, local_sem=S.sent,
                  pid=pid, routing_id=rid, dma_engine_mask=allm)
     sent = alln
 
+    order = [p[1] for p in plan] + [rank]
+    pe.wait_ge(S.selr, 1)
+    pe.wait_ge(S.ld1, 16)
+    for q in order:
+        for i in range(G):
+            pe.matmul(T["ps%d" % q][:, 0:F], T.sel[0:KP, G - 1 - i:G - 1 - i + 128],
+                      T.tab[0:KP, i * W + q * F:i * W + (q + 1) * F], i == 0, i == G - 1).then_inc(S["mm%d" % q], 1)
+
     v.wait_ge(S.ld0, 16)
-    for _w, q, _m, _n in plan[1:]:
-        v.tensor_copy(blk(T.p0, q), blk(tab(0), q)).then_inc(S.v0, 1)
-    v.wait_ge(S.ld1, 16)
-    v.tensor_copy(blk(T.p1, first), blk(tab(1), first)).then_inc(S.v1, 1)
-    v.wait_ge(S.v0, N - 2)
-    for _w, q, _m, _n in plan[1:]:
-        v.tensor_tensor(blk(T.p1, q), blk(T.p0, q), blk(tab(1), q), add).then_inc(S.v1, 1)
-    v.wait_ge(S.ld2, 16)
-    v.wait_ge(S.v1, N - 1)
-    for _w, q, _m, _n in plan:
-        v.tensor_tensor(blk(T.p2, q), blk(T.p1, q), blk(tab(2), q), add).then_inc(S.v2, 1)
-    v.wait_ge(S.ld3, 16)
-    v.wait_ge(S.v2, N - 1)
     for wave, q, _m, _n in plan:
-        v.tensor_tensor(blk(T.part, q), blk(T.p2, q), blk(tab(3), q), add).then_inc(S["rdy%d" % wave], 1)
+        v.wait_ge(S["mm%d" % q], G)
+        if q == first:
+            v.tensor_copy(blk(T.part, q), T["ps%d" % q][:, 0:F]).then_inc(S["rdy%d" % wave], 1)
+        else:
+            v.tensor_tensor(blk(T.part, q), T["ps%d" % q][:, 0:F], blk(T.t0, q), add).then_inc(S["rdy%d" % wave], 1)
 
     for wave in (0, 1):
         mine = [p for p in plan if p[0] == wave]
@@ -102,11 +114,8 @@ def rank_program(g, core, T, topo):
             sent += n
         g.remote_dma_fused(xs, local_sem=S.sent)
 
-    v.tensor_tensor(blk(T.p1, rank), blk(tab(0), rank), blk(tab(1), rank), add).then_inc(S.o1, 1)
-    v.wait_ge(S.o1, 1)
-    v.tensor_tensor(blk(T.p2, rank), blk(T.p1, rank), blk(tab(2), rank), add).then_inc(S.o2, 1)
-    v.wait_ge(S.o2, 1)
-    v.tensor_tensor(blk(T.acc, 0), blk(T.p2, rank), blk(tab(3), rank), add).then_inc(S.own, 1)
+    v.wait_ge(S["mm%d" % rank], G)
+    v.tensor_tensor(blk(T.acc, 0), T["ps%d" % rank][:, 0:F], blk(T.t0, rank), add).then_inc(S.own, 1)
 
     inc = []
     for r in range(N):

@@ -25,7 +25,7 @@ SCRATCH = {
     "land": ("sbuf", [128, (N - 1) * F], "float32"),
     "res": ("sbuf", [128, F], "float32"),
 }
-SEMAPHORES = ["ld0", "ld1", "b0", "b1", "b2", "selr", "mm0", "mm1", "mm2", "mm3", "rdy0", "rdy1", "own",
+SEMAPHORES = ["ld0", "ld1", "b0", "b1", "b2", "selr", "mm0", "mm1", "mm2", "mm3", "rdy0", "rdy1", "rdy2", "own",
               "arre", "arr0", "arr1", "arr2", "a0", "a1", "a2", "done", "stored", "sent"]
 
 
@@ -46,11 +46,9 @@ def _engines(topo, cores, r):
 
 def _plan(topo, cores, r):
     n = len(cores)
-    a, b, c = sorted([(r + d) % n for d in range(1, n)], key=lambda q: -_hops(topo, cores[r], cores[q]))
+    dsts = sorted([(r + d) % n for d in range(1, n)], key=lambda q: -_hops(topo, cores[r], cores[q]))
     eng = _engines(topo, cores, r)
-    h = len(eng) // 2
-    bits = lambda es: sum(1 << e for e in es)
-    return [(0, a, bits(eng[:h]), h), (0, c, bits(eng[h:]), len(eng) - h), (1, b, bits(eng), len(eng))]
+    return [(w, q, sum(1 << e for e in eng), len(eng)) for w, q in enumerate(dsts)]
 
 
 def rank_program(g, core, T, topo):
@@ -67,7 +65,7 @@ def rank_program(g, core, T, topo):
 
     plan = _plan(topo, cores, rank)
     first = plan[0][1]
-    allm, alln = plan[-1][2], plan[-1][3]
+    allm, alln = plan[0][2], plan[0][3]
 
     g.sync.dma_start(T.t0[:], T.gr[0]).then_inc(S.ld0, 16)
     g.scalar.dma_start(T.tab[0:KP, :], T.gr[1:K]).then_inc(S.ld1, 16)
@@ -102,17 +100,13 @@ def rank_program(g, core, T, topo):
         else:
             v.tensor_tensor(blk(T.part, q), T["ps%d" % q][:, 0:F], blk(T.t0, q), add).then_inc(S["rdy%d" % wave], 1)
 
-    for wave in (0, 1):
-        mine = [p for p in plan if p[0] == wave]
-        g.wait_ge(S["rdy%d" % wave], len(mine))
-        xs = []
-        for _w, q, m, n in mine:
-            rid, pid, _se = topo.addr(cores[q])
-            s = slot(q, rank)
-            xs.append(RemoteDMATransfer(dst_ids=[DstId(rid=rid, pnc=pid)], dma_engine_mask=m,
-                                        remote_sem=S["arr%d" % s], src=blk(T.part, q), dst=blk(T.land, s)))
-            sent += n
-        g.remote_dma_fused(xs, local_sem=S.sent)
+    for wave, q, m, n in plan:
+        rid, pid, _se = topo.addr(cores[q])
+        s = slot(q, rank)
+        g.wait_ge(S["rdy%d" % wave], 1)
+        g.remote_dma(out_ap=blk(T.land, s), in_ap=blk(T.part, q), remote_sem=S["arr%d" % s], local_sem=S.sent,
+                     pid=pid, routing_id=rid, dma_engine_mask=m)
+        sent += n
 
     v.wait_ge(S["mm%d" % rank], G)
     v.tensor_tensor(blk(T.acc, 0), T["ps%d" % rank][:, 0:F], blk(T.t0, rank), add).then_inc(S.own, 1)
@@ -122,7 +116,7 @@ def rank_program(g, core, T, topo):
         if r != rank:
             pr = _plan(topo, cores, r)
             if pr[0][1] == rank:
-                inc.append((-1, S.arre, pr[-1][3], T.early[:]))
+                inc.append((-1, S.arre, pr[0][3], T.early[:]))
             inc += [(w, S["arr%d" % slot(rank, r)], n, blk(T.land, slot(rank, r))) for w, q, _m, n in pr if q == rank]
     inc.sort(key=lambda x: x[0])
     v.wait_ge(S.own, 1)

from concourse.bass import DstId, RemoteDMATransfer
from concourse.mybir import AluOpType

N, K, F = 4, 4, 64
W = N * F
G = 4
PT = 128 // G
KP = (K - 1) * PT
WS = 128 + G - 1

SCRATCH = {
    "t0": ("sbuf", [128, W], "bfloat16"),
    "tab": ("sbuf", [128, G * W], "bfloat16"),
    "ones": ("sbuf", [128, WS], "float32"),
    "idx": ("sbuf", [128, WS], "float32"),
    "tr": ("sbuf", [128, 32], "float32"),
    "sel": ("sbuf", [128, WS], "bfloat16"),
    "ps0": ("psum", [128, 512], "float32"),
    "ps1": ("psum", [128, 512], "float32"),
    "ps2": ("psum", [128, 512], "float32"),
    "ps3": ("psum", [128, 512], "float32"),
    "part": ("sbuf", [128, W], "float32"),
    "acc": ("psum", [128, N * F], "float32"),
    "early": ("sbuf", [128, F], "bfloat16"),
    "land": ("sbuf", [128, (N - 1) * F], "float32"),
    "res": ("sbuf", [128, F], "float32"),
}
SEMAPHORES = ["ld0", "ld1", "b0", "b1", "b2", "selr", "mm0", "mm1", "mm2", "mm3", "rdy0", "rdy1", "rdy2", "own",
              "arre", "arr0", "arr1", "arr2", "a0", "a1", "a2", "done", "stored", "sent"]


def _hops(topo, a, b):
    ca, cb = topo.chip(a), topo.chip(b)
    if ca == cb:
        return 0
    return 1 if (topo.mates(ca, cb) or topo.same_plane(ca, cb)) else 2


def _engines(topo, cores, r):
    m = -1
    for q in range(len(cores)):
        if q != r:
            m &= topo.mask(cores[r], cores[q])
    return [e for e in range(m.bit_length()) if (m >> e) & 1]


def _plan(topo, cores, r):
    n = len(cores)
    dsts = sorted([(r + d) % n for d in range(1, n)], key=lambda q: -_hops(topo, cores[r], cores[q]))
    eng = _engines(topo, cores, r)
    return [(w, q, sum(1 << e for e in eng), len(eng)) for w, q in enumerate(dsts)]


def rank_program(g, core, T, topo):
    rank = T.rank_of(core)
    if rank is None:
        return
    S, cores, v, pe, add = T.sem, T.cores, g.vector, g.tensor, AluOpType.add

    def blk(t, q):
        return t[:, q * F:(q + 1) * F]

    def slot(dst, src):
        return (src - dst) % N - 1

    plan = _plan(topo, cores, rank)
    first = plan[0][1]
    allm, alln = plan[0][2], plan[0][3]

    g.sync.dma_start(T.t0[:], T.gr[0]).then_inc(S.ld0, 16)
    g.scalar.dma_start(T.tab[0:KP, :], T.gr[1:K]).then_inc(S.ld1, 16)

    v.memset(T.ones[:], 1.0).then_inc(S.b0, 1)
    v.wait_ge(S.b0, 1)
    v.tensor_tensor_scan(T.idx[:], T.ones[:], T.ones[:], 0.0, AluOpType.mult, add).then_inc(S.b1, 1)
    v.wait_ge(S.b1, 1)
    v.transpose(T.tr[:], T.idx[:, 0:32]).then_inc(S.b2, 1)
    v.wait_ge(S.b2, 1)
    v.tensor_scalar(T.sel[:], T.idx[:], 1.0 / G, T.tr[:, 0:1], AluOpType.mult, AluOpType.is_equal).then_inc(S.selr, 1)

    rid, pid, _se = topo.addr(cores[first])
    g.wait_ge(S.ld0, 16)
    g.remote_dma(out_ap=T.early[:], in_ap=blk(T.t0, first), remote_sem=S.arre, local_sem=S.sent,
                 pid=pid, routing_id=rid, dma_engine_mask=allm)
    sent = alln

    order = [p[1] for p in plan] + [rank]
    pe.wait_ge(S.selr, 1)
    pe.wait_ge(S.ld1, 16)
    for q in order:
        for i in range(G):
            pe.matmul(T["ps%d" % q][:, 0:F], T.sel[0:KP, G - 1 - i:G - 1 - i + 128],
                      T.tab[0:KP, i * W + q * F:i * W + (q + 1) * F], i == 0, i == G - 1).then_inc(S["mm%d" % q], 1)

    v.wait_ge(S.ld0, 16)
    for wave, q, _m, _n in plan:
        v.wait_ge(S["mm%d" % q], G)
        if q == first:
            v.tensor_copy(blk(T.part, q), T["ps%d" % q][:, 0:F]).then_inc(S["rdy%d" % wave], 1)
        else:
            v.tensor_tensor(blk(T.part, q), T["ps%d" % q][:, 0:F], blk(T.t0, q), add).then_inc(S["rdy%d" % wave], 1)

    for wave, q, m, n in plan:
        rid, pid, _se = topo.addr(cores[q])
        s = slot(q, rank)
        g.wait_ge(S["rdy%d" % wave], 1)
        g.remote_dma(out_ap=blk(T.land, s), in_ap=blk(T.part, q), remote_sem=S["arr%d" % s], local_sem=S.sent,
                     pid=pid, routing_id=rid, dma_engine_mask=m)
        sent += n

    v.wait_ge(S["mm%d" % rank], G)
    v.tensor_tensor(blk(T.acc, 0), T["ps%d" % rank][:, 0:F], blk(T.t0, rank), add).then_inc(S.own, 1)

    inc = []
    for r in range(N):
        if r != rank:
            pr = _plan(topo, cores, r)
            if pr[0][1] == rank:
                inc.append((-1, S.arre, pr[0][3], T.early[:]))
            inc += [(w, S["arr%d" % slot(rank, r)], n, blk(T.land, slot(rank, r))) for w, q, _m, n in pr if q == rank]
    inc.sort(key=lambda x: x[0])
    v.wait_ge(S.own, 1)
    for i, (_w, sem, n, ap) in enumerate(inc):
        v.wait_ge(sem, n)
        if i > 0:
            v.wait_ge(S["a%d" % (i - 1)], 1)
        if i < len(inc) - 1:
            v.tensor_tensor(blk(T.acc, i + 1), blk(T.acc, i), ap, add).then_inc(S["a%d" % i], 1)
        else:
            v.tensor_tensor(T.res[:], blk(T.acc, i), ap, add).then_inc(S.done, 1)
    g.sync.wait_ge(S.done, 1)
    g.sync.dma_start(T.y[:], T.res[:]).then_inc(S.stored, 16)
    g.sync.wait_ge(S.stored, 16)
    g.wait_ge(S.sent, sent)
